import numpy as np
import ml_dtypes


def mxq(x, axis, fmt="e4m3"):
    dtype, down = {"e4m3": (ml_dtypes.float8_e4m3fn, 7), "e5m2": (ml_dtypes.float8_e5m2, 14)}[fmt]
    v = np.moveaxis(np.asarray(x, np.float32).astype(ml_dtypes.bfloat16).astype(np.float64), axis, -1)
    blocks = v.reshape(v.shape[:-1] + (-1, 32))
    amax = np.abs(blocks).max(-1, keepdims=True)
    byte = np.maximum(np.where(amax > 0, np.frexp(amax)[1] - 1 + 127, 0) - down, 1)
    scale = np.exp2(byte - 127.0)
    codes = (blocks / scale).astype(np.float32).astype(dtype).astype(np.float64)
    return np.moveaxis((codes * scale).reshape(v.shape), -1, axis)


WIDE = False


def mx_kscale(k):
    if not WIDE:
        return np.ones(k)
    levels = np.array([10, -10, 5, -5, 0])
    if k % 512:
        return np.exp2(np.random.permutation(np.resize(levels, k // 32))).repeat(32)
    a = np.empty((k // 512, 16))
    for p in range(k // 512):
        a[p, :8] = np.random.permutation(np.resize(levels, 8))
        for g in range(8):
            far = levels[np.abs(levels - a[p, g]) >= 10]
            a[p, g + 8] = far[np.random.randint(len(far))]
    return np.exp2(a.ravel()).repeat(32)


def f64(x):
    return np.asarray(x).astype(np.float64)


def striped(idx):
    return np.tile(np.asarray(idx).reshape(-1, 16).T, (8, 1)).astype(np.uint16)


def unstriped(offs):
    return offs[:16].T.reshape(-1).astype(np.int64)


E2M1 = np.array([0.0, 0.5, 1.0, 1.5, 2.0, 3.0, 4.0, 6.0, -0.0, -0.5, -1.0, -1.5, -2.0, -3.0, -4.0, -6.0])


def pack_weight(w, fmt):
    k, n = w.shape
    w = f64(np.asarray(w, np.float32).astype(ml_dtypes.bfloat16)).reshape(k // 32, 32, n)
    amax = np.abs(w).max(1)
    if fmt == "e4m3":
        byte = np.frexp(amax)[1] - 1 + 127 - 7
    else:
        mant, ex = np.frexp(amax / 6.0)
        byte = np.where(mant > 0.5, ex, ex - 1) + 127
    byte = np.clip(np.where(amax > 0, byte, 1), 1, 254)
    scaled = (w * np.exp2(127.0 - byte)[:, None, :]).reshape(k, n).astype(np.float32)
    by_word = np.ascontiguousarray(scaled.reshape(k // 512, 128, 4, n).transpose(0, 1, 3, 2))
    if fmt == "e4m3":
        words = by_word.astype(ml_dtypes.float8_e4m3fn).view(np.uint8)
    else:
        c = by_word.astype(ml_dtypes.float4_e2m1fn).view(np.uint8) & 0xF
        words = (c[..., 0::2] | (c[..., 1::2] << 4)).reshape(k // 512, 128, 2 * n)
    return np.ascontiguousarray(words), np.ascontiguousarray(byte.astype(np.uint8).reshape(k // 512, 16, n))


def unpack_weight(words, scales, fmt):
    g, _, n = scales.shape
    words = np.ascontiguousarray(words).reshape(g, 128, n, -1)
    if fmt == "e4m3":
        vals = words.view(ml_dtypes.float8_e4m3fn).astype(np.float64)
    else:
        nib = np.empty((g, 128, n, 4), np.uint8)
        nib[..., 0::2] = words & 0xF
        nib[..., 1::2] = words >> 4
        vals = E2M1[nib]
    vals = vals * np.repeat(np.exp2(scales.astype(np.float64) - 127.0), 8, axis=1)[..., None]
    return vals.transpose(0, 1, 3, 2).reshape(g * 512, n)


K, T, J, N, E = 512, 1024, 256, 256, 512


def setup_inputs():
    n = np.random.standard_normal
    idx = np.random.permutation(T)[:J]
    idx2 = np.random.permutation(E)[:J]
    fk = mx_kscale(K)
    wp = pack_weight(n((K, N)) * 1 / np.sqrt(K) / fk[:, None], "e4m3")
    wdp = pack_weight((np.random.uniform(0.4, 2.0, (K, N)) / K) / fk[:, None], "e2m1")
    return {
        "ca": (np.random.randint(1, 10, (K, T)).astype(np.float64) ** 2).astype(np.float32),
        "sa": (np.random.uniform(0.1, 0.4, (K, 1)) * fk[:, None]).astype(np.float32),
        "w_words": wp[0],
        "w_scales": wp[1],
        "wd_words": wdp[0],
        "wd_scales": wdp[1],
        "so": (np.random.uniform(0.5, 1.6, (N, 1))).astype(np.float32),
        "offs": striped(idx),
        "offs2": striped(idx2),
    }


def reference(ca, sa, w_words, w_scales, wd_words, wd_scales, so, offs, offs2):
    idx = unstriped(offs)
    idx2 = unstriped(offs2)
    wu = unpack_weight(w_words, w_scales, "e4m3")
    wdu = unpack_weight(wd_words, wd_scales, "e2m1")
    z = f64(ca)[:, idx] * f64(sa)
    zq = mxq(z, 0, "e4m3")
    p = wu.T @ zq
    d = wdu.T @ zq
    m0 = p / d
    y = np.zeros((N, E))
    y[:, idx2] = m0 * f64(so)
    return y

@@ -1,0 +1,120 @@
+from contextlib import ExitStack
+
+import concourse.mybir as mybir
+
+K, T, J, N, E = 512, 1024, 256, 256, 512
+FLOPS = 2 * 2 * K * N * J
+
+F32 = mybir.dt.float32
+BF16 = mybir.dt.bfloat16
+I32 = mybir.dt.int32
+U32 = mybir.dt.uint32
+U16 = mybir.dt.uint16
+U8 = mybir.dt.uint8
+FP8X4 = mybir.dt.float8_e4m3fn_x4
+FP4X4 = mybir.dt.float4_e2m1fn_x4
+ACT = mybir.ActivationFunctionType
+MULT = mybir.AluOpType.mult
+
+P = 128
+PACK = 4
+HALF = 128
+HALVES = J // HALF
+TILES = N // P
+LIST_COLS = HALF // 16
+
+
+def tile_list_codedshare_kernel(tc, ca, sa, w_words, w_scales, wd_words, wd_scales, so, offs, offs2, out):
+    nc = tc.nc
+    with ExitStack() as ctx:
+        keep = ctx.enter_context(tc.tile_pool(name="keep", bufs=1))
+        psum = ctx.enter_context(tc.psum_pool(name="psum", bufs=1))
+
+        pick = keep.tile([P, J // 16], U16, name="pick")
+        place = keep.tile([P, J // 16], U16, name="place")
+        unit = keep.tile([P, PACK], F32, name="unit")
+        gain = keep.tile([P, TILES], F32, name="gain")
+        rows = [keep.tile([P, T], F32, name="rows%d" % r) for r in range(PACK)]
+        w_codes = keep.tile([P, N], U32, name="w_codes", align_bytes=64)
+        wd_codes = keep.tile([P, 2 * N], U8, name="wd_codes", align_bytes=64)
+        w_plane = keep.tile([P, N], U8, name="w_plane", align_bytes=64)
+        wd_plane = keep.tile([P, N], U8, name="wd_plane", align_bytes=64)
+        pages = [keep.tile([P, E], F32, name="page%d" % t) for t in range(TILES)]
+
+        for page in pages:
+            nc.vector.memset(page[:], 0.0)
+
+        ca_rows = ca.rearrange("(p r) t -> r p t", r=PACK)
+        nc.sync.dma_start(pick[:], offs)
+        nc.scalar.dma_start(unit[:], sa.rearrange("(p r) o -> p (r o)", r=PACK))
+        for r in range(PACK):
+            nc.sync.dma_start(rows[r][:], ca_rows[r])
+        nc.sync.dma_start(wd_codes[:].bitcast(I32), wd_words[0].bitcast(I32))
+        nc.sync.dma_start(w_codes[:].bitcast(I32), w_words[0].rearrange("p n t -> p (n t)").bitcast(I32))
+        for q in range(4):
+            nc.sync.dma_start(wd_plane[32 * q : 32 * q + 4, :].bitcast(I32), wd_scales[0, 4 * q : 4 * q + 4, :].bitcast(I32))
+        nc.sync.dma_start(place[:], offs2)
+        for q in range(4):
+            nc.gpsimd.dma_start(w_plane[32 * q : 32 * q + 4, :].bitcast(I32), w_scales[0, 4 * q : 4 * q + 4, :].bitcast(I32))
+        with nc.allow_non_contiguous_dma(reason="one weight for each output row"):
+            nc.sync.dma_start(gain[:], so.rearrange("(t p) o -> p (t o)", p=P))
+
+        z = [keep.tile([P, PACK * HALF], BF16, name="z%d" % h, align_bytes=64) for h in range(HALVES)]
+        for r in range(PACK):
+            for h in range(HALVES):
+                nc.scalar.activation(
+                    out=z[h][:, r : PACK * HALF : PACK],
+                    in_=rows[r][:].indirect(pick[:, h * LIST_COLS : (h + 1) * LIST_COLS]),
+                    func=ACT.Copy,
+                    scale=unit[:, r : r + 1],
+                )
+
+        quotients = []
+        for h in range(HALVES):
+            z_codes = keep.tile([P, HALF], U32, name="z_codes%d" % h, align_bytes=64)
+            z_plane = keep.tile([P, HALF], U8, name="z_plane%d" % h, align_bytes=64)
+            nc.vector.quantize_mx(out=z_codes[:].bitcast(FP8X4), scales=z_plane[:], in_=z[h][:])
+            den = psum.tile([P, TILES * HALF], F32, name="den%d" % h)
+            num = psum.tile([P, TILES * HALF], F32, name="num%d" % h)
+            for t in range(TILES):
+                nc.tensor.matmul_mx(
+                    out=den[:, t * HALF : (t + 1) * HALF],
+                    lhsT=wd_codes[:, 2 * t * P : 2 * (t + 1) * P].bitcast(FP4X4),
+                    lhsT_scale=wd_plane[:, t * P : (t + 1) * P],
+                    rhs=z_codes[:].bitcast(FP8X4),
+                    rhs_scale=z_plane[:],
+                    start=True,
+                    stop=True,
+                )
+            for t in range(TILES):
+                nc.tensor.matmul_mx(
+                    out=num[:, t * HALF : (t + 1) * HALF],
+                    lhsT=w_codes[:, t * P : (t + 1) * P].bitcast(FP8X4),
+                    lhsT_scale=w_plane[:, t * P : (t + 1) * P],
+                    rhs=z_codes[:].bitcast(FP8X4),
+                    rhs_scale=z_plane[:],
+                    start=True,
+                    stop=True,
+                )
+            sign = keep.tile([P, TILES * HALF], F32, name="sign%d" % h)
+            root = keep.tile([P, TILES * HALF], F32, name="root%d" % h)
+            nc.scalar.activation(out=sign[:], in_=den[:], func=ACT.Sign)
+            nc.scalar.activation(out=root[:], in_=den[:], func=ACT.Abs_reciprocal_sqrt)
+            signed = keep.tile([P, TILES * HALF], F32, name="signed%d" % h)
+            halfway = keep.tile([P, TILES * HALF], F32, name="halfway%d" % h)
+            quotient = keep.tile([P, TILES * HALF], F32, name="quotient%d" % h)
+            nc.vector.tensor_tensor(signed[:], num[:], sign[:], MULT)
+            nc.vector.tensor_tensor(halfway[:], signed[:], root[:], MULT)
+            nc.vector.tensor_tensor(quotient[:], halfway[:], root[:], MULT)
+            quotients.append(quotient)
+
+        for h in range(HALVES):
+            for t in range(TILES):
+                nc.scalar.activation(
+                    out=pages[t][:].indirect(place[:, h * LIST_COLS : (h + 1) * LIST_COLS]),
+                    in_=quotients[h][:, t * HALF : (t + 1) * HALF],
+                    func=ACT.Copy,
+                    scale=gain[:, t : t + 1],
+                )
+        for t in range(TILES):
+            nc.sync.dma_start(out[t * P : (t + 1) * P, :], pages[t][:])

@@ -41,6 +41,10 @@ def tile_list_codedshare_kernel(tc, ca, sa, w_words, w_scales, wd_words, wd_scal
         wd_plane = keep.tile([P, N], U8, name="wd_plane", align_bytes=64)
         pages = [keep.tile([P, E], F32, name="page%d" % t) for t in range(TILES)]
 
+        warm_in = keep.tile([P, 1], F32, name="warm_in")
+        warm_out = keep.tile([P, 1], F32, name="warm_out")
+        nc.vector.memset(warm_in[:], 1.0)
+        nc.scalar.activation(out=warm_out[:], in_=warm_in[:], func=ACT.Abs_reciprocal_sqrt)
         for page in pages:
             nc.vector.memset(page[:], 0.0)
 

@@ -41,6 +41,27 @@ def tile_list_codedshare_kernel(tc, ca, sa, w_words, w_scales, wd_words, wd_scal
         wd_plane = keep.tile([P, N], U8, name="wd_plane", align_bytes=64)
         pages = [keep.tile([P, E], F32, name="page%d" % t) for t in range(TILES)]
 
+        def load_scales(engine, plane, scales, q):
+            engine.dma_start(plane[32 * q : 32 * q + 4, :].bitcast(I32), scales[0, 4 * q : 4 * q + 4, :].bitcast(I32))
+
+        ca_rows = ca.rearrange("(p r) t -> r p t", r=PACK)
+        nc.sync.dma_start(pick[:], offs)
+        nc.scalar.dma_start(unit[:], sa.rearrange("(p r) o -> p (r o)", r=PACK))
+        for q in range(3):
+            load_scales(nc.scalar, wd_plane, wd_scales, q)
+        load_scales(nc.gpsimd, wd_plane, wd_scales, 3)
+        load_scales(nc.gpsimd, w_plane, w_scales, 3)
+        with nc.allow_non_contiguous_dma(reason="one weight for each output row"):
+            nc.gpsimd.dma_start(gain[:], so.rearrange("(t p) o -> p (t o)", p=P))
+        for r in range(PACK - 1):
+            nc.sync.dma_start(rows[r][:], ca_rows[r])
+        for q in range(3):
+            load_scales(nc.sync, w_plane, w_scales, q)
+        nc.sync.dma_start(rows[PACK - 1][:], ca_rows[PACK - 1])
+        nc.sync.dma_start(wd_codes[:].bitcast(I32), wd_words[0].bitcast(I32))
+        nc.sync.dma_start(w_codes[:].bitcast(I32), w_words[0].rearrange("p n t -> p (n t)").bitcast(I32))
+        nc.sync.dma_start(place[:], offs2)
+
         warm_in = keep.tile([P, 1], F32, name="warm_in")
         warm_out = keep.tile([P, 1], F32, name="warm_out")
         nc.vector.memset(warm_in[:], 1.0)
@@ -48,75 +69,63 @@ def tile_list_codedshare_kernel(tc, ca, sa, w_words, w_scales, wd_words, wd_scal
         for page in pages:
             nc.vector.memset(page[:], 0.0)
 
-        ca_rows = ca.rearrange("(p r) t -> r p t", r=PACK)
-        nc.sync.dma_start(pick[:], offs)
-        nc.scalar.dma_start(unit[:], sa.rearrange("(p r) o -> p (r o)", r=PACK))
-        for r in range(PACK):
-            nc.sync.dma_start(rows[r][:], ca_rows[r])
-        nc.sync.dma_start(wd_codes[:].bitcast(I32), wd_words[0].bitcast(I32))
-        nc.sync.dma_start(w_codes[:].bitcast(I32), w_words[0].rearrange("p n t -> p (n t)").bitcast(I32))
-        for q in range(4):
-            nc.sync.dma_start(wd_plane[32 * q : 32 * q + 4, :].bitcast(I32), wd_scales[0, 4 * q : 4 * q + 4, :].bitcast(I32))
-        nc.sync.dma_start(place[:], offs2)
-        for q in range(4):
-            nc.gpsimd.dma_start(w_plane[32 * q : 32 * q + 4, :].bitcast(I32), w_scales[0, 4 * q : 4 * q + 4, :].bitcast(I32))
-        with nc.allow_non_contiguous_dma(reason="one weight for each output row"):
-            nc.sync.dma_start(gain[:], so.rearrange("(t p) o -> p (t o)", p=P))
-
         z = [keep.tile([P, PACK * HALF], BF16, name="z%d" % h, align_bytes=64) for h in range(HALVES)]
-        for r in range(PACK):
-            for h in range(HALVES):
-                nc.scalar.activation(
-                    out=z[h][:, r : PACK * HALF : PACK],
-                    in_=rows[r][:].indirect(pick[:, h * LIST_COLS : (h + 1) * LIST_COLS]),
-                    func=ACT.Copy,
-                    scale=unit[:, r : r + 1],
-                )
+        for r, h in [(r, h) for r in range(PACK) for h in range(HALVES)]:
+            nc.scalar.activation(
+                out=z[h][:, r : PACK * HALF : PACK],
+                in_=rows[r][:].indirect(pick[:, h * LIST_COLS : (h + 1) * LIST_COLS]),
+                func=ACT.Copy,
+                scale=unit[:, r : r + 1],
+            )
 
-        quotients = []
+        z_codes = [keep.tile([P, HALF], U32, name="z_codes%d" % h, align_bytes=64) for h in range(HALVES)]
+        z_plane = [keep.tile([P, HALF], U8, name="z_plane%d" % h, align_bytes=64) for h in range(HALVES)]
         for h in range(HALVES):
-            z_codes = keep.tile([P, HALF], U32, name="z_codes%d" % h, align_bytes=64)
-            z_plane = keep.tile([P, HALF], U8, name="z_plane%d" % h, align_bytes=64)
-            nc.vector.quantize_mx(out=z_codes[:].bitcast(FP8X4), scales=z_plane[:], in_=z[h][:])
-            den = psum.tile([P, TILES * HALF], F32, name="den%d" % h)
-            num = psum.tile([P, TILES * HALF], F32, name="num%d" % h)
-            for t in range(TILES):
+            nc.vector.quantize_mx(out=z_codes[h][:].bitcast(FP8X4), scales=z_plane[h][:], in_=z[h][:])
+
+        quotients = {}
+        for u, (h, tiles) in enumerate([(0, (0,)), (0, (1,)), (1, (0, 1))]):
+            width = len(tiles) * HALF
+            den = psum.tile([P, width], F32, name="den%d" % u)
+            num = psum.tile([P, width], F32, name="num%d" % u)
+            for i, t in enumerate(tiles):
                 nc.tensor.matmul_mx(
-                    out=den[:, t * HALF : (t + 1) * HALF],
+                    out=den[:, i * HALF : (i + 1) * HALF],
                     lhsT=wd_codes[:, 2 * t * P : 2 * (t + 1) * P].bitcast(FP4X4),
                     lhsT_scale=wd_plane[:, t * P : (t + 1) * P],
-                    rhs=z_codes[:].bitcast(FP8X4),
-                    rhs_scale=z_plane[:],
+                    rhs=z_codes[h][:].bitcast(FP8X4),
+                    rhs_scale=z_plane[h][:],
                     start=True,
                     stop=True,
                 )
-            for t in range(TILES):
+            for i, t in enumerate(tiles):
                 nc.tensor.matmul_mx(
-                    out=num[:, t * HALF : (t + 1) * HALF],
+                    out=num[:, i * HALF : (i + 1) * HALF],
                     lhsT=w_codes[:, t * P : (t + 1) * P].bitcast(FP8X4),
                     lhsT_scale=w_plane[:, t * P : (t + 1) * P],
-                    rhs=z_codes[:].bitcast(FP8X4),
-                    rhs_scale=z_plane[:],
+                    rhs=z_codes[h][:].bitcast(FP8X4),
+                    rhs_scale=z_plane[h][:],
                     start=True,
                     stop=True,
                 )
-            sign = keep.tile([P, TILES * HALF], F32, name="sign%d" % h)
-            root = keep.tile([P, TILES * HALF], F32, name="root%d" % h)
-            nc.scalar.activation(out=sign[:], in_=den[:], func=ACT.Sign)
+            sign = keep.tile([P, width], F32, name="sign%d" % u)
+            root = keep.tile([P, width], F32, name="root%d" % u)
             nc.scalar.activation(out=root[:], in_=den[:], func=ACT.Abs_reciprocal_sqrt)
-            signed = keep.tile([P, TILES * HALF], F32, name="signed%d" % h)
-            halfway = keep.tile([P, TILES * HALF], F32, name="halfway%d" % h)
-            quotient = keep.tile([P, TILES * HALF], F32, name="quotient%d" % h)
+            nc.scalar.activation(out=sign[:], in_=den[:], func=ACT.Sign)
+            inverse = keep.tile([P, width], F32, name="inverse%d" % u)
+            signed = keep.tile([P, width], F32, name="signed%d" % u)
+            quotient = keep.tile([P, width], F32, name="quotient%d" % u)
+            nc.vector.tensor_tensor(inverse[:], root[:], root[:], MULT)
             nc.vector.tensor_tensor(signed[:], num[:], sign[:], MULT)
-            nc.vector.tensor_tensor(halfway[:], signed[:], root[:], MULT)
-            nc.vector.tensor_tensor(quotient[:], halfway[:], root[:], MULT)
-            quotients.append(quotient)
+            nc.vector.tensor_tensor(quotient[:], signed[:], inverse[:], MULT)
+            for i, t in enumerate(tiles):
+                quotients[h, t] = quotient[:, i * HALF : (i + 1) * HALF]
 
         for h in range(HALVES):
             for t in range(TILES):
                 nc.scalar.activation(
                     out=pages[t][:].indirect(place[:, h * LIST_COLS : (h + 1) * LIST_COLS]),
-                    in_=quotients[h][:, t * HALF : (t + 1) * HALF],
+                    in_=quotients[h, t],
                     func=ACT.Copy,
                     scale=gain[:, t : t + 1],
                 )

@@ -22,6 +22,7 @@ HALF = 128
 HALVES = J // HALF
 TILES = N // P
 LIST_COLS = HALF // 16
+LEAD = 64
 
 
 def tile_list_codedshare_kernel(tc, ca, sa, w_words, w_scales, wd_words, wd_scales, so, offs, offs2, out):
@@ -45,22 +46,23 @@ def tile_list_codedshare_kernel(tc, ca, sa, w_words, w_scales, wd_words, wd_scal
             engine.dma_start(plane[32 * q : 32 * q + 4, :].bitcast(I32), scales[0, 4 * q : 4 * q + 4, :].bitcast(I32))
 
         ca_rows = ca.rearrange("(p r) t -> r p t", r=PACK)
-        nc.sync.dma_start(pick[:], offs)
+        nc.sync.dma_start(rows[0][:], ca_rows[0])
         nc.scalar.dma_start(unit[:], sa.rearrange("(p r) o -> p (r o)", r=PACK))
-        for q in range(3):
+        nc.sync.dma_start(pick[:], offs)
+        for q in range(2):
             load_scales(nc.scalar, wd_plane, wd_scales, q)
         load_scales(nc.gpsimd, wd_plane, wd_scales, 3)
         load_scales(nc.gpsimd, w_plane, w_scales, 3)
-        with nc.allow_non_contiguous_dma(reason="one weight for each output row"):
-            nc.gpsimd.dma_start(gain[:], so.rearrange("(t p) o -> p (t o)", p=P))
-        for r in range(PACK - 1):
+        for r in range(1, PACK):
             nc.sync.dma_start(rows[r][:], ca_rows[r])
+        load_scales(nc.sync, wd_plane, wd_scales, 2)
         for q in range(3):
             load_scales(nc.sync, w_plane, w_scales, q)
-        nc.sync.dma_start(rows[PACK - 1][:], ca_rows[PACK - 1])
         nc.sync.dma_start(wd_codes[:].bitcast(I32), wd_words[0].bitcast(I32))
         nc.sync.dma_start(w_codes[:].bitcast(I32), w_words[0].rearrange("p n t -> p (n t)").bitcast(I32))
         nc.sync.dma_start(place[:], offs2)
+        with nc.allow_non_contiguous_dma(reason="one weight for each output row"):
+            nc.sync.dma_start(gain[:], so.rearrange("(t p) o -> p (t o)", p=P))
 
         warm_in = keep.tile([P, 1], F32, name="warm_in")
         warm_out = keep.tile([P, 1], F32, name="warm_out")
@@ -83,51 +85,63 @@ def tile_list_codedshare_kernel(tc, ca, sa, w_words, w_scales, wd_words, wd_scal
         for h in range(HALVES):
             nc.vector.quantize_mx(out=z_codes[h][:].bitcast(FP8X4), scales=z_plane[h][:], in_=z[h][:])
 
-        quotients = {}
-        for u, (h, tiles) in enumerate([(0, (0,)), (0, (1,)), (1, (0, 1))]):
-            width = len(tiles) * HALF
-            den = psum.tile([P, width], F32, name="den%d" % u)
-            num = psum.tile([P, width], F32, name="num%d" % u)
-            for i, t in enumerate(tiles):
-                nc.tensor.matmul_mx(
-                    out=den[:, i * HALF : (i + 1) * HALF],
-                    lhsT=wd_codes[:, 2 * t * P : 2 * (t + 1) * P].bitcast(FP4X4),
-                    lhsT_scale=wd_plane[:, t * P : (t + 1) * P],
-                    rhs=z_codes[h][:].bitcast(FP8X4),
-                    rhs_scale=z_plane[h][:],
-                    start=True,
-                    stop=True,
-                )
-            for i, t in enumerate(tiles):
-                nc.tensor.matmul_mx(
-                    out=num[:, i * HALF : (i + 1) * HALF],
-                    lhsT=w_codes[:, t * P : (t + 1) * P].bitcast(FP8X4),
-                    lhsT_scale=w_plane[:, t * P : (t + 1) * P],
-                    rhs=z_codes[h][:].bitcast(FP8X4),
-                    rhs_scale=z_plane[h][:],
-                    start=True,
-                    stop=True,
-                )
-            sign = keep.tile([P, width], F32, name="sign%d" % u)
-            root = keep.tile([P, width], F32, name="root%d" % u)
-            nc.scalar.activation(out=root[:], in_=den[:], func=ACT.Abs_reciprocal_sqrt)
-            nc.scalar.activation(out=sign[:], in_=den[:], func=ACT.Sign)
-            inverse = keep.tile([P, width], F32, name="inverse%d" % u)
-            signed = keep.tile([P, width], F32, name="signed%d" % u)
-            quotient = keep.tile([P, width], F32, name="quotient%d" % u)
-            nc.vector.tensor_tensor(inverse[:], root[:], root[:], MULT)
-            nc.vector.tensor_tensor(signed[:], num[:], sign[:], MULT)
-            nc.vector.tensor_tensor(quotient[:], signed[:], inverse[:], MULT)
-            for i, t in enumerate(tiles):
-                quotients[h, t] = quotient[:, i * HALF : (i + 1) * HALF]
+        def product(acc, codes, plane, fmt, width, t, h):
+            nc.tensor.matmul_mx(
+                out=acc,
+                lhsT=codes[:, width * t : width * (t + 1)].bitcast(fmt),
+                lhsT_scale=plane[:, t * P : (t + 1) * P],
+                rhs=z_codes[h][:].bitcast(FP8X4),
+                rhs_scale=z_plane[h][:],
+                start=True,
+                stop=True,
+            )
 
-        for h in range(HALVES):
-            for t in range(TILES):
-                nc.scalar.activation(
-                    out=pages[t][:].indirect(place[:, h * LIST_COLS : (h + 1) * LIST_COLS]),
-                    in_=quotients[h, t],
-                    func=ACT.Copy,
-                    scale=gain[:, t : t + 1],
-                )
+        def divide(name, num, den, width):
+            root = keep.tile([P, width], F32, name="root" + name)
+            sign = keep.tile([P, width], F32, name="sign" + name)
+            inverse = keep.tile([P, width], F32, name="inverse" + name)
+            signed = keep.tile([P, width], F32, name="signed" + name)
+            quotient = keep.tile([P, width], F32, name="quotient" + name)
+            nc.scalar.activation(out=root[:], in_=den, func=ACT.Abs_reciprocal_sqrt)
+            nc.scalar.activation(out=sign[:], in_=den, func=ACT.Sign)
+            nc.vector.tensor_tensor(inverse[:], root[:], root[:], MULT)
+            nc.vector.tensor_tensor(signed[:], num, sign[:], MULT)
+            nc.vector.tensor_tensor(quotient[:], signed[:], inverse[:], MULT)
+            return quotient
+
+        def put(t, first, count, values):
+            nc.scalar.activation(
+                out=pages[t][:].indirect(place[:, first // 16 : (first + count) // 16]),
+                in_=values,
+                func=ACT.Copy,
+                scale=gain[:, t : t + 1],
+            )
+
+        den0 = [psum.tile([P, HALF], F32, name="den0_%d" % t) for t in range(TILES)]
+        num0 = [psum.tile([P, HALF], F32, name="num0_%d" % t) for t in range(TILES)]
+        den1 = psum.tile([P, TILES * HALF], F32, name="den1")
+        num1 = psum.tile([P, TILES * HALF], F32, name="num1")
         for t in range(TILES):
+            product(den0[t][:], wd_codes, wd_plane, FP4X4, 2 * P, t, 0)
+        for t in range(TILES):
+            product(num0[t][:], w_codes, w_plane, FP8X4, P, t, 0)
+        for t in range(TILES):
+            product(den1[:, t * HALF : (t + 1) * HALF], wd_codes, wd_plane, FP4X4, 2 * P, t, 1)
+        for t in range(TILES):
+            product(num1[:, t * HALF : (t + 1) * HALF], w_codes, w_plane, FP8X4, P, t, 1)
+
+        lead_inverse = keep.tile([P, LEAD], F32, name="lead_inverse")
+        lead = keep.tile([P, LEAD], F32, name="lead")
+        nc.vector.reciprocal(lead_inverse[:], den0[0][:, :LEAD])
+        nc.vector.tensor_tensor(lead[:], num0[0][:, :LEAD], lead_inverse[:], MULT)
+        second = divide("b", num0[1][:], den0[1][:], HALF)
+        third = divide("a", num0[0][:, LEAD:], den0[0][:, LEAD:], HALF - LEAD)
+        last = divide("c", num1[:], den1[:], TILES * HALF)
+
+        put(0, 0, LEAD, lead[:])
+        put(1, 0, HALF, second[:])
+        put(0, LEAD, HALF - LEAD, third[:])
+        put(1, HALF, HALF, last[:, HALF:])
+        put(0, HALF, HALF, last[:, :HALF])
+        for t in (1, 0):
             nc.sync.dma_start(out[t * P : (t + 1) * P, :], pages[t][:])

@@ -49,14 +49,12 @@ def tile_list_codedshare_kernel(tc, ca, sa, w_words, w_scales, wd_words, wd_scal
         nc.sync.dma_start(rows[0][:], ca_rows[0])
         nc.scalar.dma_start(unit[:], sa.rearrange("(p r) o -> p (r o)", r=PACK))
         nc.sync.dma_start(pick[:], offs)
-        for q in range(2):
+        for q in range(3):
             load_scales(nc.scalar, wd_plane, wd_scales, q)
-        load_scales(nc.gpsimd, wd_plane, wd_scales, 3)
-        load_scales(nc.gpsimd, w_plane, w_scales, 3)
         for r in range(1, PACK):
             nc.sync.dma_start(rows[r][:], ca_rows[r])
-        load_scales(nc.sync, wd_plane, wd_scales, 2)
-        for q in range(3):
+        load_scales(nc.sync, wd_plane, wd_scales, 3)
+        for q in range(4):
             load_scales(nc.sync, w_plane, w_scales, q)
         nc.sync.dma_start(wd_codes[:].bitcast(I32), wd_words[0].bitcast(I32))
         nc.sync.dma_start(w_codes[:].bitcast(I32), w_words[0].rearrange("p n t -> p (n t)").bitcast(I32))

from contextlib import ExitStack

import concourse.mybir as mybir

K, T, J, N, E = 512, 1024, 256, 256, 512
FLOPS = 2 * 2 * K * N * J

F32 = mybir.dt.float32
BF16 = mybir.dt.bfloat16
I32 = mybir.dt.int32
U32 = mybir.dt.uint32
U16 = mybir.dt.uint16
U8 = mybir.dt.uint8
FP8X4 = mybir.dt.float8_e4m3fn_x4
FP4X4 = mybir.dt.float4_e2m1fn_x4
ACT = mybir.ActivationFunctionType
MULT = mybir.AluOpType.mult

P = 128
PACK = 4
HALF = 128
HALVES = J // HALF
TILES = N // P
LIST_COLS = HALF // 16
LEAD = 64


def tile_list_codedshare_kernel(tc, ca, sa, w_words, w_scales, wd_words, wd_scales, so, offs, offs2, out):
    nc = tc.nc
    with ExitStack() as ctx:
        keep = ctx.enter_context(tc.tile_pool(name="keep", bufs=1))
        psum = ctx.enter_context(tc.psum_pool(name="psum", bufs=1))

        pick = keep.tile([P, J // 16], U16, name="pick")
        place = keep.tile([P, J // 16], U16, name="place")
        unit = keep.tile([P, PACK], F32, name="unit")
        gain = keep.tile([P, TILES], F32, name="gain")
        rows = [keep.tile([P, T], F32, name="rows%d" % r) for r in range(PACK)]
        w_codes = keep.tile([P, N], U32, name="w_codes", align_bytes=64)
        wd_codes = keep.tile([P, 2 * N], U8, name="wd_codes", align_bytes=64)
        w_plane = keep.tile([P, N], U8, name="w_plane", align_bytes=64)
        wd_plane = keep.tile([P, N], U8, name="wd_plane", align_bytes=64)
        pages = [keep.tile([P, E], F32, name="page%d" % t) for t in range(TILES)]

        def load_scales(engine, plane, scales, q):
            engine.dma_start(plane[32 * q : 32 * q + 4, :].bitcast(I32), scales[0, 4 * q : 4 * q + 4, :].bitcast(I32))

        ca_rows = ca.rearrange("(p r) t -> r p t", r=PACK)
        nc.sync.dma_start(rows[0][:], ca_rows[0])
        nc.scalar.dma_start(unit[:], sa.rearrange("(p r) o -> p (r o)", r=PACK))
        nc.sync.dma_start(pick[:], offs)
        for q in range(3):
            load_scales(nc.scalar, wd_plane, wd_scales, q)
        for r in range(1, PACK):
            nc.sync.dma_start(rows[r][:], ca_rows[r])
        load_scales(nc.sync, wd_plane, wd_scales, 3)
        for q in range(4):
            load_scales(nc.sync, w_plane, w_scales, q)
        nc.sync.dma_start(wd_codes[:].bitcast(I32), wd_words[0].bitcast(I32))
        nc.sync.dma_start(w_codes[:].bitcast(I32), w_words[0].rearrange("p n t -> p (n t)").bitcast(I32))
        nc.sync.dma_start(place[:], offs2)
        with nc.allow_non_contiguous_dma(reason="one weight for each output row"):
            nc.sync.dma_start(gain[:], so.rearrange("(t p) o -> p (t o)", p=P))

        warm_in = keep.tile([P, 1], F32, name="warm_in")
        warm_out = keep.tile([P, 1], F32, name="warm_out")
        nc.vector.memset(warm_in[:], 1.0)
        nc.scalar.activation(out=warm_out[:], in_=warm_in[:], func=ACT.Abs_reciprocal_sqrt)
        for page in pages:
            nc.vector.memset(page[:], 0.0)

        z = [keep.tile([P, PACK * HALF], BF16, name="z%d" % h, align_bytes=64) for h in range(HALVES)]
        for r, h in [(r, h) for r in range(PACK) for h in range(HALVES)]:
            nc.scalar.activation(
                out=z[h][:, r : PACK * HALF : PACK],
                in_=rows[r][:].indirect(pick[:, h * LIST_COLS : (h + 1) * LIST_COLS]),
                func=ACT.Copy,
                scale=unit[:, r : r + 1],
            )

        z_codes = [keep.tile([P, HALF], U32, name="z_codes%d" % h, align_bytes=64) for h in range(HALVES)]
        z_plane = [keep.tile([P, HALF], U8, name="z_plane%d" % h, align_bytes=64) for h in range(HALVES)]
        for h in range(HALVES):
            nc.vector.quantize_mx(out=z_codes[h][:].bitcast(FP8X4), scales=z_plane[h][:], in_=z[h][:])

        def product(acc, codes, plane, fmt, width, t, h):
            nc.tensor.matmul_mx(
                out=acc,
                lhsT=codes[:, width * t : width * (t + 1)].bitcast(fmt),
                lhsT_scale=plane[:, t * P : (t + 1) * P],
                rhs=z_codes[h][:].bitcast(FP8X4),
                rhs_scale=z_plane[h][:],
                start=True,
                stop=True,
            )

        def divide(name, num, den, width):
            root = keep.tile([P, width], F32, name="root" + name)
            sign = keep.tile([P, width], F32, name="sign" + name)
            inverse = keep.tile([P, width], F32, name="inverse" + name)
            signed = keep.tile([P, width], F32, name="signed" + name)
            quotient = keep.tile([P, width], F32, name="quotient" + name)
            nc.scalar.activation(out=root[:], in_=den, func=ACT.Abs_reciprocal_sqrt)
            nc.scalar.activation(out=sign[:], in_=den, func=ACT.Sign)
            nc.vector.tensor_tensor(inverse[:], root[:], root[:], MULT)
            nc.vector.tensor_tensor(signed[:], num, sign[:], MULT)
            nc.vector.tensor_tensor(quotient[:], signed[:], inverse[:], MULT)
            return quotient

        def put(t, first, count, values):
            nc.scalar.activation(
                out=pages[t][:].indirect(place[:, first // 16 : (first + count) // 16]),
                in_=values,
                func=ACT.Copy,
                scale=gain[:, t : t + 1],
            )

        den0 = [psum.tile([P, HALF], F32, name="den0_%d" % t) for t in range(TILES)]
        num0 = [psum.tile([P, HALF], F32, name="num0_%d" % t) for t in range(TILES)]
        den1 = psum.tile([P, TILES * HALF], F32, name="den1")
        num1 = psum.tile([P, TILES * HALF], F32, name="num1")
        for t in range(TILES):
            product(den0[t][:], wd_codes, wd_plane, FP4X4, 2 * P, t, 0)
        for t in range(TILES):
            product(num0[t][:], w_codes, w_plane, FP8X4, P, t, 0)
        for t in range(TILES):
            product(den1[:, t * HALF : (t + 1) * HALF], wd_codes, wd_plane, FP4X4, 2 * P, t, 1)
        for t in range(TILES):
            product(num1[:, t * HALF : (t + 1) * HALF], w_codes, w_plane, FP8X4, P, t, 1)

        lead_inverse = keep.tile([P, LEAD], F32, name="lead_inverse")
        lead = keep.tile([P, LEAD], F32, name="lead")
        nc.vector.reciprocal(lead_inverse[:], den0[0][:, :LEAD])
        nc.vector.tensor_tensor(lead[:], num0[0][:, :LEAD], lead_inverse[:], MULT)
        second = divide("b", num0[1][:], den0[1][:], HALF)
        third = divide("a", num0[0][:, LEAD:], den0[0][:, LEAD:], HALF - LEAD)
        last = divide("c", num1[:], den1[:], TILES * HALF)

        put(0, 0, LEAD, lead[:])
        put(1, 0, HALF, second[:])
        put(0, LEAD, HALF - LEAD, third[:])
        put(1, HALF, HALF, last[:, HALF:])
        put(0, HALF, HALF, last[:, :HALF])
        for t in (1, 0):
            nc.sync.dma_start(out[t * P : (t + 1) * P, :], pages[t][:])
